import numpy as np
import ml_dtypes


def mxq(x, axis, fmt="e4m3"):
    dtype, down = {"e4m3": (ml_dtypes.float8_e4m3fn, 7), "e5m2": (ml_dtypes.float8_e5m2, 14)}[fmt]
    v = np.moveaxis(np.asarray(x, np.float32).astype(ml_dtypes.bfloat16).astype(np.float64), axis, -1)
    blocks = v.reshape(v.shape[:-1] + (-1, 32))
    amax = np.abs(blocks).max(-1, keepdims=True)
    byte = np.maximum(np.where(amax > 0, np.frexp(amax)[1] - 1 + 127, 0) - down, 1)
    scale = np.exp2(byte - 127.0)
    codes = (blocks / scale).astype(np.float32).astype(dtype).astype(np.float64)
    return np.moveaxis((codes * scale).reshape(v.shape), -1, axis)


WIDE = False


def mx_kscale(k):
    if not WIDE:
        return np.ones(k)
    levels = np.array([10, -10, 5, -5, 0])
    if k % 512:
        return np.exp2(np.random.permutation(np.resize(levels, k // 32))).repeat(32)
    a = np.empty((k // 512, 16))
    for p in range(k // 512):
        a[p, :8] = np.random.permutation(np.resize(levels, 8))
        for g in range(8):
            far = levels[np.abs(levels - a[p, g]) >= 10]
            a[p, g + 8] = far[np.random.randint(len(far))]
    return np.exp2(a.ravel()).repeat(32)


def f64(x):
    return np.asarray(x).astype(np.float64)


def striped(idx):
    return np.tile(idx.reshape(-1, 16).T, (8, 1)).astype(np.uint16)


def unstriped(offs):
    return offs[:16].T.reshape(-1).astype(np.int64)


E2M1 = np.array([0.0, 0.5, 1.0, 1.5, 2.0, 3.0, 4.0, 6.0, -0.0, -0.5, -1.0, -1.5, -2.0, -3.0, -4.0, -6.0])


def pack_weight(w, fmt):
    k, n = w.shape
    w = f64(np.asarray(w, np.float32).astype(ml_dtypes.bfloat16)).reshape(k // 32, 32, n)
    amax = np.abs(w).max(1)
    if fmt == "e4m3":
        byte = np.frexp(amax)[1] - 1 + 127 - 7
    else:
        mant, ex = np.frexp(amax / 6.0)
        byte = np.where(mant > 0.5, ex, ex - 1) + 127
    byte = np.clip(np.where(amax > 0, byte, 1), 1, 254)
    scaled = (w * np.exp2(127.0 - byte)[:, None, :]).reshape(k, n).astype(np.float32)
    by_word = np.ascontiguousarray(scaled.reshape(k // 512, 128, 4, n).transpose(0, 1, 3, 2))
    if fmt == "e4m3":
        words = by_word.astype(ml_dtypes.float8_e4m3fn).view(np.uint8)
    else:
        c = by_word.astype(ml_dtypes.float4_e2m1fn).view(np.uint8) & 0xF
        words = (c[..., 0::2] | (c[..., 1::2] << 4)).reshape(k // 512, 128, 2 * n)
    return np.ascontiguousarray(words), np.ascontiguousarray(byte.astype(np.uint8).reshape(k // 512, 16, n))


def unpack_weight(words, scales, fmt):
    g, _, n = scales.shape
    words = np.ascontiguousarray(words).reshape(g, 128, n, -1)
    if fmt == "e4m3":
        vals = words.view(ml_dtypes.float8_e4m3fn).astype(np.float64)
    else:
        nib = np.empty((g, 128, n, 4), np.uint8)
        nib[..., 0::2] = words & 0xF
        nib[..., 1::2] = words >> 4
        vals = E2M1[nib]
    vals = vals * np.repeat(np.exp2(scales.astype(np.float64) - 127.0), 8, axis=1)[..., None]
    return vals.transpose(0, 1, 3, 2).reshape(g * 512, n)


def gelu(v):
    return 0.5 * v * (1.0 + np.tanh(np.sqrt(2.0 / np.pi) * (v + 0.044715 * v**3)))


def bf(x):
    return np.asarray(x, np.float32).astype(ml_dtypes.bfloat16)


def planes(Y):
    n, m = Y.shape
    b = f64(bf(Y)).reshape(n // 32, 32, m)
    amax = np.abs(b).max(1)
    byte = np.clip(np.where(amax > 0, np.frexp(amax)[1] - 1 + 127 - 7, 1), 1, 254)
    codes = (b * np.exp2(127.0 - byte)[:, None, :]).reshape(n, m).astype(np.float32).astype(ml_dtypes.float8_e4m3fn).view(np.uint8)
    words = codes.reshape(n // 512, 128, 4, m).transpose(0, 1, 3, 2)
    return np.ascontiguousarray(words), np.ascontiguousarray(byte.astype(np.uint8).reshape(n // 512, 16, m))


K, T, S, H, T2, P = 1024, 2048, 512, 1024, 1024, 512

def setup_inputs():
    n = np.random.standard_normal
    s, u = mx_kscale(K)[:, None], mx_kscale(H)[:, None]
    e = np.exp(0.8 * n(H))
    d = {}
    d["tab_words"], d["tab_scales"] = pack_weight(n((K, T)) * s, "e4m3")
    d["offs"] = striped(np.random.permutation(T)[:S])
    d["w1"] = (n((K, H)) / K**0.5 / s * u.T).astype(np.float32)
    d["wgs"] = np.exp(0.3 * n((128, S))).astype(np.float32)
    d["page0"] = (n((H, T2)) * u).astype(np.float32)
    d["offs2"] = striped(np.random.permutation(T2)[:S])
    d["offs3"] = striped(np.random.permutation(T2)[:P])
    d["offs4"] = striped(np.random.permutation(T2)[:P])
    d["gx"] = (np.random.uniform(0.9, 1.9, H) / u[:, 0]).astype(np.float32)
    d["gt"] = (np.random.uniform(0.6, 1.4, H) * u[:, 0]).astype(np.float32)
    d["w2_words"], d["w2_scales"] = pack_weight(1.8 * n((H, H)) / H**0.5 / u, "e2m1")
    d["gz"] = (np.random.uniform(0.3, 0.9, H) * u[:, 0]).astype(np.float32)
    d["w3"] = (n((H, H)) / H**0.5 / u * e).astype(np.float32)
    d["go"] = (np.random.uniform(0.7, 1.6, H) * e / u[:, 0]).astype(np.float32)
    return d

def reference(tab_words, tab_scales, offs, w1, wgs, page0, offs2, offs3, offs4, gx, gt, w2_words, w2_scales, gz, w3, go):
    v = unpack_weight(tab_words, tab_scales, "e4m3")[:, unstriped(offs)]
    h = mxq(f64(w1), 0, "e4m3").T @ v
    page = f64(page0).copy()
    page[:, unstriped(offs2)] = np.tile(f64(wgs), (H // 128, 1)) * h
    x = f64(gx)[:, None] * page[:, unstriped(offs3)]
    t = f64(gt)[:, None] * np.tanh(x)
    w2 = unpack_weight(w2_words, w2_scales, "e2m1")
    z = f64(gz)[:, None] * ((w2.T @ mxq(t, 0, "e4m3")) + x)
    b = mxq(f64(w3), 0, "e4m3").T @ mxq(z, 0, "e4m3")
    y = np.maximum(b, f64(go)[:, None] * page[:, unstriped(offs4)])
    words, scales = planes(y)
    return y, words, scales

@@ -1,0 +1,378 @@
+from contextlib import ExitStack
+
+import concourse.mybir as mybir
+
+K, T, S, H, T2 = 1024, 2048, 512, 1024, 1024
+FLOPS = 3 * 2 * H * H * S
+
+F32 = mybir.dt.float32
+BF16 = mybir.dt.bfloat16
+I32 = mybir.dt.int32
+U32 = mybir.dt.uint32
+U16 = mybir.dt.uint16
+U8 = mybir.dt.uint8
+FP8X4 = mybir.dt.float8_e4m3fn_x4
+FP4X4 = mybir.dt.float4_e2m1fn_x4
+ALU = mybir.AluOpType
+ACT = mybir.ActivationFunctionType
+
+P = 128
+PACK = 4
+GROUP = P * PACK
+SLOTS = H // P
+
+
+def tile_list_gore_ledger_rigging_kernel(
+    tc, tab_words, tab_scales, offs, w1, wgs, page0, offs2, offs3, offs4,
+    gx, gt, w2_words, w2_scales, gz, w3, go, out_0, out_1, out_2,
+):
+    nc = tc.nc
+    with ExitStack() as ctx:
+        lists = ctx.enter_context(tc.tile_pool(name="lists", bufs=1))
+        sb = ctx.enter_context(tc.tile_pool(name="sb", bufs=1))
+        psum = ctx.enter_context(tc.psum_pool(name="psum", bufs=1))
+
+        def new(shape, dtype, name, tag=None):
+            return sb.tile(shape, dtype, name=name, tag=tag or name, align_bytes=64)
+
+        def bank(k, name):
+            return psum.tile([P, S], F32, name=name, tag="bank%d" % k)
+
+        def load_list(src, name):
+            dst = lists.tile([P, S // 16], U16, name=name)
+            nc.sync.dma_start(dst[:], src)
+            return dst
+
+        def load_weight(w, b, a, tag, parts=1):
+            raw = new([P, PACK, GROUP], F32, "raw_%s_%d%d" % (tag, b, a), tag)
+            src = w[a * GROUP:(a + 1) * GROUP, b * GROUP:(b + 1) * GROUP].rearrange("(p i) c -> p i c", i=PACK)
+            step = PACK // parts
+            for i in range(0, PACK, step):
+                nc.sync.dma_start(raw[:, i:i + step, :], src[:, i:i + step, :])
+            return raw
+
+        def round_weight(raw, name, tag):
+            dealt = new([P, PACK, P, PACK], BF16, name, tag)
+            nc.scalar.copy(
+                dealt[:].rearrange("p t m i -> p m i t"),
+                raw[:].rearrange("p i (m t) -> p m i t", t=PACK),
+            )
+            return dealt
+
+        def quantize(src, name, tag=None, scales=None):
+            codes = new([P, GROUP], U32, name + "_codes", tag)
+            if scales is None:
+                scales = new([P, GROUP], U8, name + "_scales")[:]
+            nc.vector.quantize_mx(codes[:].bitcast(FP8X4), scales, src)
+            return codes, scales
+
+        def quantize_weight(dealt, name, tag=None):
+            return quantize(dealt[:].rearrange("p t m i -> p (t m i)"), name, tag)
+
+        def weave(src, name, tag):
+            woven = new([P, S, PACK], BF16, name, tag)
+            nc.scalar.copy(
+                woven[:].rearrange("p (c i) t -> p c t i", i=4),
+                src[:].rearrange("p t (c i) -> p c t i", i=4),
+            )
+            return woven[:].rearrange("p j t -> p (j t)")
+
+        def load_page(k):
+            b, t = divmod(k, PACK)
+            page = new([P, T2], F32, "page%d" % k)
+            rows = page0[b * GROUP:(b + 1) * GROUP, :].rearrange("(p t) c -> p t c", t=PACK)
+            nc.sync.dma_start(page[:], rows[:, t, :])
+            return page
+
+        def load_wgs(t0, t1):
+            dst = new([P, t1 - t0, S], F32, "wgs%d" % t0)
+            rows = wgs.rearrange("(p t) j -> p t j", t=PACK)
+            for q in range(4):
+                nc.sync.dma_start(dst[32 * q:32 * (q + 1), :, :], rows[:, t0:t1, :])
+            return dst
+
+        def load_gain(vec, name):
+            dst = new([P, 2, PACK], F32, name)
+            nc.sync.dma_start(dst[:], vec.rearrange("(b p t) -> p b t", p=P, t=PACK))
+            return dst
+
+        def col(gain, k):
+            b, t = divmod(k, PACK)
+            return gain[:, b, t:t + 1]
+
+        tab_s = new([P, T], U8, "tab_s")
+        nc.vector.memset(tab_s[:].bitcast(I32), 0)
+        w2_s_raw = new([P, 2, H], U8, "w2_s_raw")
+        nc.vector.memset(w2_s_raw[:].rearrange("p a c -> p (a c)").bitcast(I32), 0)
+
+        tab_w = [new([P, T], U32, "tab_w%d" % a) for a in range(2)]
+
+        def load_tab(a, half):
+            cols = slice(half * T // 2, (half + 1) * T // 2)
+            nc.sync.dma_start(
+                tab_w[a][:, cols].bitcast(I32),
+                tab_words[a].rearrange("p n t -> p (n t)").bitcast(I32)[:, cols],
+            )
+
+        raw1 = {}
+        raw3 = {}
+        pages = {}
+        raw1[0, 0] = load_weight(w1, 0, 0, "stage0", 2)
+        raw1[0, 1] = load_weight(w1, 0, 1, "stage1", 2)
+        idx = load_list(offs, "idx")
+        load_tab(0, 0)
+        load_tab(0, 1)
+        load_tab(1, 0)
+        for q in range(4):
+            nc.sync.dma_start(
+                tab_s[32 * q:32 * q + 8, :].bitcast(I32),
+                tab_scales[:, 4 * q:4 * q + 4, :].bitcast(I32),
+            )
+        load_tab(1, 1)
+        wg0 = load_wgs(0, 1)
+        idx2 = load_list(offs2, "idx2")
+        pages[0] = load_page(0)
+        pages[1] = load_page(1)
+        wg1 = load_wgs(1, 2)
+        idx3 = load_list(offs3, "idx3")
+        raw1[1, 0] = load_weight(w1, 1, 0, "stage2")
+        gx_t = load_gain(gx, "gx_t")
+        gt_t = load_gain(gt, "gt_t")
+        gz_t = load_gain(gz, "gz_t")
+        raw1[1, 1] = load_weight(w1, 1, 1, "stage3")
+        pages[2] = load_page(2)
+        pages[3] = load_page(3)
+        wg2 = load_wgs(2, 4)
+        wg = [wg0[:, 0, :], wg1[:, 0, :], wg2[:, 0, :], wg2[:, 1, :]]
+        for k in range(PACK, SLOTS):
+            pages[k] = load_page(k)
+
+        q1 = {}
+        q3 = {}
+        for a in range(2):
+            q1[0, a] = quantize_weight(round_weight(raw1[0, a], "w1d_0%d" % a, "dealt%d" % a), "w1_0%d" % a)
+        raw3[0, 0] = load_weight(w3, 0, 0, "stage0")
+        raw3[0, 1] = load_weight(w3, 0, 1, "stage1")
+        w2_w_raw = new([P, 2, 2 * H], U8, "w2_w_raw")
+        nc.sync.dma_start(w2_w_raw[:].bitcast(I32), w2_words.rearrange("a p c -> p a c").bitcast(I32))
+        for q in range(4):
+            nc.sync.dma_start(
+                w2_s_raw[32 * q:32 * q + 4, :, :].bitcast(I32),
+                w2_scales[:, 4 * q:4 * q + 4, :].rearrange("a r c -> r a c").bitcast(I32),
+            )
+        idx4 = load_list(offs4, "idx4")
+        go_t = load_gain(go, "go_t")
+
+        w2_s = new([P, 2, H], U8, "w2_s")
+        nc.vector.tensor_copy(
+            w2_s[:].rearrange("p a (b t o i) -> p (a b) o t i", b=2, t=PACK, i=16),
+            w2_s_raw[:].rearrange("p a (b o i t) -> p (a b) o t i", b=2, t=PACK, i=16),
+        )
+
+        v_w = []
+        v_s = new([P, S], U8, "v_s")
+        for a in range(2):
+            words = new([P, S], U32, "v_w%d" % a)
+            nc.vector.tensor_copy(words[:], tab_w[a][:].indirect(idx[:]))
+            v_w.append(words)
+            if a == 0:
+                nc.vector.tensor_copy(v_s[:], tab_s[:].indirect(idx[:]))
+
+        h = {}
+
+        def stage1(k):
+            b, t = divmod(k, PACK)
+            acc = bank(k, "h_acc%d" % k)
+            cols = slice(t * P, (t + 1) * P)
+            order = (0, 1) if k == 0 else (1, 0)
+            for a in order:
+                codes, scales = q1[b, a]
+                nc.tensor.matmul_mx(
+                    acc[:], lhsT=codes[:, cols].bitcast(FP8X4), lhsT_scale=scales[:, cols],
+                    rhs=v_w[a][:].bitcast(FP8X4), rhs_scale=v_s[4 * a:P, :],
+                    start=(a == order[0]), stop=(a == order[1]),
+                )
+            h[k] = new([P, S], F32, "h%d" % k)
+            nc.scalar.copy(h[k][:], acc[:])
+
+        picked = {}
+        t_rows = [new([P, PACK, S], BF16, "t_rows%d" % b, "rows%d" % b) for b in range(2)]
+
+        def put(k):
+            nc.vector.tensor_tensor(pages[k][:].indirect(idx2[:]), h[k][:], wg[k % PACK], ALU.mult)
+
+        def pick(k):
+            picked[k] = new([P, S], F32, "picked%d" % k)
+            nc.vector.tensor_copy(picked[k][:], pages[k][:].indirect(idx3[:]))
+
+        def gate(k, tag):
+            b, t = divmod(k, PACK)
+            th = new([P, S], F32, "th%d" % k, tag)
+            nc.scalar.activation(th[:], picked[k][:], ACT.Tanh, scale=col(gx_t, k))
+            nc.scalar.activation(t_rows[b][:, t, :], th[:], ACT.Copy, scale=col(gt_t, k))
+
+        def skip(k):
+            nc.scalar.activation(picked[k][:], picked[k][:], ACT.Copy, scale=col(gxz_t, k))
+
+        for k in range(PACK):
+            stage1(k)
+
+        opposite = [new([P, PACK * S], F32, "opposite%d" % b) for b in range(2)]
+
+        def weave_into(src, half):
+            b, u = divmod(half, 2)
+            dst = opposite[b][:, 2 * u * S:2 * (u + 1) * S].bitcast(BF16)
+            nc.scalar.copy(
+                dst.rearrange("p (c i t) -> p c t i", i=4, t=PACK),
+                src[:].rearrange("p t (c i) -> p c t i", i=4),
+            )
+            return dst
+
+        d10 = round_weight(raw1[1, 0], "w1d_10", "dealt0")
+        d11 = round_weight(raw1[1, 1], "w1d_11", "dealt1")
+        put(0)
+        put(1)
+        pick(0)
+        pick(1)
+        gxz_t = new([P, 2, PACK], F32, "gxz_t")
+        nc.vector.tensor_tensor(gxz_t[:], gx_t[:], gz_t[:], ALU.mult)
+        q1[1, 0] = quantize_weight(d10, "w1_10")
+        q1[1, 1] = quantize_weight(d11, "w1_11")
+        gate(0, "stage2")
+        skip(0)
+        raw3[1, 0] = load_weight(w3, 1, 0, "stage2")
+        gate(1, "stage3")
+        skip(1)
+        raw3[1, 1] = load_weight(w3, 1, 1, "stage3")
+        for k in range(PACK, SLOTS):
+            stage1(k)
+        put(2)
+        put(3)
+        pick(2)
+        pick(3)
+        d3a = round_weight(raw3[0, 0], "w3d_00", "dealt0")
+        gate(2, "stage0")
+        skip(2)
+        d3b = round_weight(raw3[0, 1], "w3d_01", "dealt1")
+        gate(3, "stage1")
+        t_woven0 = weave_into(t_rows[0], 0)
+        skip(3)
+        w2_w = new([P, 2, 2 * H], U8, "w2_w", "stage1")
+        nc.scalar.copy(
+            w2_w[:].bitcast(U16).rearrange("p a (b t o i) -> p (a b) o t i", b=2, t=PACK, i=8),
+            w2_w_raw[:].bitcast(U16).rearrange("p a (b o i t) -> p (a b) o t i", b=2, t=PACK, i=8),
+        )
+        put(4)
+        put(5)
+        pick(4)
+        gate(4, "w2_w_raw")
+        skip(4)
+        d3c = round_weight(raw3[1, 0], "w3d_10", "dealt2")
+        put(6)
+        pick(5)
+        gate(5, "stage2")
+        skip(5)
+        put(7)
+        pick(6)
+        pick(7)
+        gate(6, "stage2")
+        gate(7, "stage2")
+        t_woven1 = weave_into(t_rows[1], 1)
+        skip(6)
+        skip(7)
+        d3d = round_weight(raw3[1, 1], "w3d_11", "rows1")
+        qt = [quantize(t_woven0, "t0")]
+        q3[0, 0] = quantize_weight(d3a, "w3_00")
+        q3[0, 1] = quantize_weight(d3b, "w3_01")
+
+        def pick_opposite(k):
+            b, t = divmod(k, PACK)
+            nc.vector.tensor_copy(opposite[b][:, t * S:(t + 1) * S], pages[k][:].indirect(idx4[:]))
+
+        s_acc = [bank(k, "s_acc%d" % k) for k in range(SLOTS)]
+
+        def stage2(k, a):
+            codes, scales = qt[a]
+            nc.tensor.matmul_mx(
+                s_acc[k][:], lhsT=w2_w[:, a, 2 * k * P:2 * (k + 1) * P].bitcast(FP4X4),
+                lhsT_scale=w2_s[:, a, k * P:(k + 1) * P],
+                rhs=codes[:].bitcast(FP8X4), rhs_scale=scales,
+                start=(a == 0), stop=(a == 1),
+            )
+
+        for k in range(SLOTS):
+            stage2(k, 0)
+        pick_opposite(0)
+        pick_opposite(1)
+        qt.append(quantize(t_woven1, "t1"))
+        q3[1, 0] = quantize_weight(d3c, "w3_10")
+        pick_opposite(2)
+        pick_opposite(3)
+        for k in range(SLOTS):
+            stage2(k, 1)
+
+        z_rows = [new([P, PACK, S], BF16, "z_rows0", "rows0"), new([P, PACK, S], BF16, "z_rows1")]
+        z_woven = []
+        for b in range(2):
+            for t in range(PACK):
+                k = b * PACK + t
+                nc.vector.scalar_tensor_tensor(
+                    z_rows[b][:, t, :], s_acc[k][:], col(gz_t, k), picked[k][:], ALU.mult, ALU.add,
+                )
+            z_woven.append(weave_into(z_rows[b], 2 + b))
+
+        y_acc = [bank(k, "y_acc%d" % k) for k in range(SLOTS)]
+        qz = []
+
+        def stage3(k, a):
+            b, t = divmod(k, PACK)
+            cols = slice(t * P, (t + 1) * P)
+            codes, scales = q3[b, a]
+            nc.tensor.matmul_mx(
+                y_acc[k][:], lhsT=codes[:, cols].bitcast(FP8X4), lhsT_scale=scales[:, cols],
+                rhs=qz[a][0][:].bitcast(FP8X4), rhs_scale=qz[a][1],
+                start=(a == 0), stop=(a == 1),
+            )
+
+        for a in range(2):
+            qz.append(quantize(z_woven[a], "z%d" % a))
+            if a == 0:
+                q3[1, 1] = quantize_weight(d3d, "w3_11")
+            for k in range(SLOTS):
+                stage3(k, a)
+        for k in range(PACK, SLOTS):
+            pick_opposite(k)
+
+        y_scales = new([P, 2, S], U8, "y_scales")
+        y_codes = [new([P, S], U32, "y_codes%d" % b) for b in range(2)]
+
+        def finish(b, j0, j1, engine_copy, tag):
+            rows = out_0[b * GROUP:(b + 1) * GROUP, :].rearrange("(p t) j -> p t j", t=PACK)
+            y = opposite[b][:].rearrange("p (t j) -> p t j", t=PACK)[:, :, j0:j1]
+            for t in range(PACK):
+                k = b * PACK + t
+                nc.vector.scalar_tensor_tensor(
+                    y[:, t, :], y[:, t, :], col(go_t, k), y_acc[k][:, j0:j1], ALU.mult, ALU.max)
+                if j1 - j0 == S:
+                    nc.sync.dma_start(rows[:, t, :], y[:, t, :])
+            if j1 - j0 < S:
+                nc.sync.dma_start(rows[:, :, j0:j1], y)
+            woven = new([P, j1 - j0, PACK], BF16, "y_woven%d_%d" % (b, j0), tag)
+            engine_copy(
+                woven[:].rearrange("p (c i) t -> p c t i", i=4),
+                y.rearrange("p t (c i) -> p c t i", i=4),
+            )
+            nc.vector.quantize_mx(
+                y_codes[b][:, j0:j1].bitcast(FP8X4), y_scales[:, b, j0:j1],
+                woven[:].rearrange("p j t -> p (j t)"))
+            nc.sync.dma_start(
+                out_1[b].rearrange("p m t -> p (m t)").bitcast(I32)[:, j0:j1], y_codes[b][:, j0:j1].bitcast(I32))
+
+        finish(0, 0, S, nc.scalar.copy, "woven0")
+        finish(1, 0, S // 2, nc.scalar.copy, "woven1")
+        finish(1, S // 2, S, nc.vector.tensor_copy, "woven2")
+        for q in range(4):
+            nc.sync.dma_start(
+                out_2[:, 4 * q:4 * q + 4, :].rearrange("g r m -> r g m").bitcast(I32),
+                y_scales[32 * q:32 * q + 4, :, :].bitcast(I32),
+            )

@@ -43,12 +43,10 @@ def tile_list_gore_ledger_rigging_kernel(
             nc.sync.dma_start(dst[:], src)
             return dst
 
-        def load_weight(w, b, a, tag, parts=1):
+        def load_weight(w, b, a, tag):
             raw = new([P, PACK, GROUP], F32, "raw_%s_%d%d" % (tag, b, a), tag)
             src = w[a * GROUP:(a + 1) * GROUP, b * GROUP:(b + 1) * GROUP].rearrange("(p i) c -> p i c", i=PACK)
-            step = PACK // parts
-            for i in range(0, PACK, step):
-                nc.sync.dma_start(raw[:, i:i + step, :], src[:, i:i + step, :])
+            nc.sync.dma_start(raw[:], src)
             return raw
 
         def round_weight(raw, name, tag):
@@ -69,13 +67,12 @@ def tile_list_gore_ledger_rigging_kernel(
         def quantize_weight(dealt, name, tag=None):
             return quantize(dealt[:].rearrange("p t m i -> p (t m i)"), name, tag)
 
-        def weave(src, name, tag):
-            woven = new([P, S, PACK], BF16, name, tag)
+        def weave(src, dst):
             nc.scalar.copy(
-                woven[:].rearrange("p (c i) t -> p c t i", i=4),
-                src[:].rearrange("p t (c i) -> p c t i", i=4),
+                dst.rearrange("p (c i t) -> p c t i", i=4, t=PACK),
+                src.rearrange("p (t c i) -> p c t i", i=4, t=PACK),
             )
-            return woven[:].rearrange("p j t -> p (j t)")
+            return dst
 
         def load_page(k):
             b, t = divmod(k, PACK)
@@ -87,7 +84,7 @@ def tile_list_gore_ledger_rigging_kernel(
         def load_wgs(t0, t1):
             dst = new([P, t1 - t0, S], F32, "wgs%d" % t0)
             rows = wgs.rearrange("(p t) j -> p t j", t=PACK)
-            for q in range(4):
+            for q in (0, 2, 1, 3):
                 nc.sync.dma_start(dst[32 * q:32 * (q + 1), :, :], rows[:, t0:t1, :])
             return dst
 
@@ -100,6 +97,12 @@ def tile_list_gore_ledger_rigging_kernel(
             b, t = divmod(k, PACK)
             return gain[:, b, t:t + 1]
 
+        def entries(u):
+            return slice(u * S // 2, (u + 1) * S // 2)
+
+        def columns(u):
+            return slice(u * S // 32, (u + 1) * S // 32)
+
         tab_s = new([P, T], U8, "tab_s")
         nc.vector.memset(tab_s[:].bitcast(I32), 0)
         w2_s_raw = new([P, 2, H], U8, "w2_s_raw")
@@ -107,43 +110,42 @@ def tile_list_gore_ledger_rigging_kernel(
 
         tab_w = [new([P, T], U32, "tab_w%d" % a) for a in range(2)]
 
-        def load_tab(a, half):
-            cols = slice(half * T // 2, (half + 1) * T // 2)
+        def load_tab(a):
             nc.sync.dma_start(
-                tab_w[a][:, cols].bitcast(I32),
-                tab_words[a].rearrange("p n t -> p (n t)").bitcast(I32)[:, cols],
+                tab_w[a][:].bitcast(I32),
+                tab_words[a].rearrange("p n t -> p (n t)").bitcast(I32),
             )
 
         raw1 = {}
         raw3 = {}
         pages = {}
-        raw1[0, 0] = load_weight(w1, 0, 0, "stage0", 2)
-        raw1[0, 1] = load_weight(w1, 0, 1, "stage1", 2)
-        idx = load_list(offs, "idx")
-        load_tab(0, 0)
-        load_tab(0, 1)
-        load_tab(1, 0)
+        raw1[0, 0] = load_weight(w1, 0, 0, "stage0")
+        tab_s_rows = new([P, T // 4], I32, "tab_s_rows")
         for q in range(4):
-            nc.sync.dma_start(
-                tab_s[32 * q:32 * q + 8, :].bitcast(I32),
-                tab_scales[:, 4 * q:4 * q + 4, :].bitcast(I32),
-            )
-        load_tab(1, 1)
-        wg0 = load_wgs(0, 1)
+            live = slice(32 * q, 32 * q + 8)
+            nc.sync.dma_start(tab_s_rows[live, :], tab_scales[:, 4 * q:4 * q + 4, :].bitcast(I32))
+            nc.vector.tensor_copy(tab_s[live, :].bitcast(I32), tab_s_rows[live, :])
+        idx = load_list(offs, "idx")
+        raw1[0, 1] = load_weight(w1, 0, 1, "stage1")
+        load_tab(0)
+        load_tab(1)
         idx2 = load_list(offs2, "idx2")
+        wg0 = load_wgs(0, 1)
         pages[0] = load_page(0)
         pages[1] = load_page(1)
         wg1 = load_wgs(1, 2)
         idx3 = load_list(offs3, "idx3")
         raw1[1, 0] = load_weight(w1, 1, 0, "stage2")
         gx_t = load_gain(gx, "gx_t")
+        raw1[1, 1] = load_weight(w1, 1, 1, "stage3")
         gt_t = load_gain(gt, "gt_t")
         gz_t = load_gain(gz, "gz_t")
-        raw1[1, 1] = load_weight(w1, 1, 1, "stage3")
         pages[2] = load_page(2)
         pages[3] = load_page(3)
         wg2 = load_wgs(2, 4)
         wg = [wg0[:, 0, :], wg1[:, 0, :], wg2[:, 0, :], wg2[:, 1, :]]
+        w2_w_raw = new([P, 2, 2 * H], U8, "w2_w_raw")
+        nc.sync.dma_start(w2_w_raw[:].bitcast(I32), w2_words.rearrange("a p c -> p a c").bitcast(I32))
         for k in range(PACK, SLOTS):
             pages[k] = load_page(k)
 
@@ -153,15 +155,13 @@ def tile_list_gore_ledger_rigging_kernel(
             q1[0, a] = quantize_weight(round_weight(raw1[0, a], "w1d_0%d" % a, "dealt%d" % a), "w1_0%d" % a)
         raw3[0, 0] = load_weight(w3, 0, 0, "stage0")
         raw3[0, 1] = load_weight(w3, 0, 1, "stage1")
-        w2_w_raw = new([P, 2, 2 * H], U8, "w2_w_raw")
-        nc.sync.dma_start(w2_w_raw[:].bitcast(I32), w2_words.rearrange("a p c -> p a c").bitcast(I32))
+        idx4 = load_list(offs4, "idx4")
+        go_t = load_gain(go, "go_t")
         for q in range(4):
             nc.sync.dma_start(
                 w2_s_raw[32 * q:32 * q + 4, :, :].bitcast(I32),
                 w2_scales[:, 4 * q:4 * q + 4, :].rearrange("a r c -> r a c").bitcast(I32),
             )
-        idx4 = load_list(offs4, "idx4")
-        go_t = load_gain(go, "go_t")
 
         w2_s = new([P, 2, H], U8, "w2_s")
         nc.vector.tensor_copy(
@@ -173,30 +173,43 @@ def tile_list_gore_ledger_rigging_kernel(
         v_s = new([P, S], U8, "v_s")
         for a in range(2):
             words = new([P, S], U32, "v_w%d" % a)
-            nc.vector.tensor_copy(words[:], tab_w[a][:].indirect(idx[:]))
             v_w.append(words)
-            if a == 0:
-                nc.vector.tensor_copy(v_s[:], tab_s[:].indirect(idx[:]))
+        nc.vector.tensor_copy(v_s[:], tab_s[:].indirect(idx[:]))
+        nc.vector.tensor_copy(v_w[0][:], tab_w[0][:].indirect(idx[:]))
+        for u in range(2):
+            nc.vector.tensor_copy(v_w[1][:, entries(u)], tab_w[1][:].indirect(idx[:, columns(u)]))
 
         h = {}
 
-        def stage1(k):
+        def stage1_part(k, acc, js, order):
             b, t = divmod(k, PACK)
-            acc = bank(k, "h_acc%d" % k)
             cols = slice(t * P, (t + 1) * P)
-            order = (0, 1) if k == 0 else (1, 0)
             for a in order:
                 codes, scales = q1[b, a]
                 nc.tensor.matmul_mx(
-                    acc[:], lhsT=codes[:, cols].bitcast(FP8X4), lhsT_scale=scales[:, cols],
-                    rhs=v_w[a][:].bitcast(FP8X4), rhs_scale=v_s[4 * a:P, :],
+                    acc, lhsT=codes[:, cols].bitcast(FP8X4), lhsT_scale=scales[:, cols],
+                    rhs=v_w[a][:, js].bitcast(FP8X4), rhs_scale=v_s[4 * a:P, js],
                     start=(a == order[0]), stop=(a == order[1]),
                 )
+            nc.scalar.copy(h[k][:, js], acc)
+
+        def stage1(k):
             h[k] = new([P, S], F32, "h%d" % k)
-            nc.scalar.copy(h[k][:], acc[:])
+            if k == 0:
+                for u in range(2):
+                    acc = bank(u * (SLOTS - 1), "h_acc0_%d" % u)
+                    stage1_part(0, acc[:, 0:S // 2], entries(u), (0, 1))
+            else:
+                stage1_part(k, bank(k, "h_acc%d" % k)[:], slice(0, S), (1, 0))
 
         picked = {}
-        t_rows = [new([P, PACK, S], BF16, "t_rows%d" % b, "rows%d" % b) for b in range(2)]
+        opposite = [new([P, PACK * S], F32, "opposite%d" % b) for b in range(2)]
+
+        def lodge(half):
+            b, u = divmod(half, 2)
+            return opposite[b][:, 2 * u * S:2 * (u + 1) * S].bitcast(BF16)
+
+        t_rows = [lodge(0), new([P, PACK * S], BF16, "t_rows1", "rows1")[:]]
 
         def put(k):
             nc.vector.tensor_tensor(pages[k][:].indirect(idx2[:]), h[k][:], wg[k % PACK], ALU.mult)
@@ -209,7 +222,7 @@ def tile_list_gore_ledger_rigging_kernel(
             b, t = divmod(k, PACK)
             th = new([P, S], F32, "th%d" % k, tag)
             nc.scalar.activation(th[:], picked[k][:], ACT.Tanh, scale=col(gx_t, k))
-            nc.scalar.activation(t_rows[b][:, t, :], th[:], ACT.Copy, scale=col(gt_t, k))
+            nc.scalar.activation(t_rows[b][:, t * S:(t + 1) * S], th[:], ACT.Copy, scale=col(gt_t, k))
 
         def skip(k):
             nc.scalar.activation(picked[k][:], picked[k][:], ACT.Copy, scale=col(gxz_t, k))
@@ -217,20 +230,11 @@ def tile_list_gore_ledger_rigging_kernel(
         for k in range(PACK):
             stage1(k)
 
-        opposite = [new([P, PACK * S], F32, "opposite%d" % b) for b in range(2)]
-
-        def weave_into(src, half):
-            b, u = divmod(half, 2)
-            dst = opposite[b][:, 2 * u * S:2 * (u + 1) * S].bitcast(BF16)
-            nc.scalar.copy(
-                dst.rearrange("p (c i t) -> p c t i", i=4, t=PACK),
-                src[:].rearrange("p t (c i) -> p c t i", i=4),
-            )
-            return dst
-
         d10 = round_weight(raw1[1, 0], "w1d_10", "dealt0")
         d11 = round_weight(raw1[1, 1], "w1d_11", "dealt1")
-        put(0)
+        for u in range(2):
+            nc.vector.tensor_tensor(
+                pages[0][:].indirect(idx2[:, columns(u)]), h[0][:, entries(u)], wg[0][:, entries(u)], ALU.mult)
         put(1)
         pick(0)
         pick(1)
@@ -244,6 +248,11 @@ def tile_list_gore_ledger_rigging_kernel(
         gate(1, "stage3")
         skip(1)
         raw3[1, 1] = load_weight(w3, 1, 1, "stage3")
+        w2_w = new([P, 2, 2 * H], U8, "w2_w")
+        nc.scalar.copy(
+            w2_w[:].bitcast(U16).rearrange("p a (b t o i) -> p (a b) o t i", b=2, t=PACK, i=8),
+            w2_w_raw[:].bitcast(U16).rearrange("p a (b o i t) -> p (a b) o t i", b=2, t=PACK, i=8),
+        )
         for k in range(PACK, SLOTS):
             stage1(k)
         put(2)
@@ -253,32 +262,27 @@ def tile_list_gore_ledger_rigging_kernel(
         d3a = round_weight(raw3[0, 0], "w3d_00", "dealt0")
         gate(2, "stage0")
         skip(2)
-        d3b = round_weight(raw3[0, 1], "w3d_01", "dealt1")
-        gate(3, "stage1")
-        t_woven0 = weave_into(t_rows[0], 0)
+        gate(3, "stage0")
+        t_woven0 = weave(t_rows[0], new([P, PACK * S], BF16, "t_woven0", "woven0")[:])
         skip(3)
-        w2_w = new([P, 2, 2 * H], U8, "w2_w", "stage1")
-        nc.scalar.copy(
-            w2_w[:].bitcast(U16).rearrange("p a (b t o i) -> p (a b) o t i", b=2, t=PACK, i=8),
-            w2_w_raw[:].bitcast(U16).rearrange("p a (b o i t) -> p (a b) o t i", b=2, t=PACK, i=8),
-        )
+        d3b = round_weight(raw3[0, 1], "w3d_01", "stage0")
         put(4)
         put(5)
         pick(4)
-        gate(4, "w2_w_raw")
+        gate(4, "stage1")
         skip(4)
-        d3c = round_weight(raw3[1, 0], "w3d_10", "dealt2")
         put(6)
         pick(5)
-        gate(5, "stage2")
+        gate(5, "stage1")
         skip(5)
+        d3c = round_weight(raw3[1, 0], "w3d_10", "stage1")
         put(7)
         pick(6)
         pick(7)
         gate(6, "stage2")
-        gate(7, "stage2")
-        t_woven1 = weave_into(t_rows[1], 1)
         skip(6)
+        gate(7, "stage2")
+        t_woven1 = weave(t_rows[1], lodge(1))
         skip(7)
         d3d = round_weight(raw3[1, 1], "w3d_11", "rows1")
         qt = [quantize(t_woven0, "t0")]
@@ -304,22 +308,24 @@ def tile_list_gore_ledger_rigging_kernel(
             stage2(k, 0)
         pick_opposite(0)
         pick_opposite(1)
-        qt.append(quantize(t_woven1, "t1"))
         q3[1, 0] = quantize_weight(d3c, "w3_10")
+        qt.append(quantize(t_woven1, "t1"))
         pick_opposite(2)
         pick_opposite(3)
         for k in range(SLOTS):
             stage2(k, 1)
 
-        z_rows = [new([P, PACK, S], BF16, "z_rows0", "rows0"), new([P, PACK, S], BF16, "z_rows1")]
+        z_rows = [lodge(2), lodge(3)]
         z_woven = []
         for b in range(2):
             for t in range(PACK):
                 k = b * PACK + t
                 nc.vector.scalar_tensor_tensor(
-                    z_rows[b][:, t, :], s_acc[k][:], col(gz_t, k), picked[k][:], ALU.mult, ALU.add,
+                    z_rows[b][:, t * S:(t + 1) * S], s_acc[k][:], col(gz_t, k), picked[k][:], ALU.mult, ALU.add,
                 )
-            z_woven.append(weave_into(z_rows[b], 2 + b))
+            z_woven.append(weave(z_rows[b], new([P, PACK * S], BF16, "z_woven%d" % b, "woven%d" % b)[:]))
+
+        q3[1, 1] = quantize_weight(d3d, "w3_11")
 
         y_acc = [bank(k, "y_acc%d" % k) for k in range(SLOTS)]
         qz = []
@@ -336,8 +342,6 @@ def tile_list_gore_ledger_rigging_kernel(
 
         for a in range(2):
             qz.append(quantize(z_woven[a], "z%d" % a))
-            if a == 0:
-                q3[1, 1] = quantize_weight(d3d, "w3_11")
             for k in range(SLOTS):
                 stage3(k, a)
         for k in range(PACK, SLOTS):

@@ -57,20 +57,20 @@ def tile_list_gore_ledger_rigging_kernel(
             )
             return dealt
 
-        def quantize(src, name, tag=None, scales=None):
-            codes = new([P, GROUP], U32, name + "_codes", tag)
-            if scales is None:
-                scales = new([P, GROUP], U8, name + "_scales")[:]
-            nc.vector.quantize_mx(codes[:].bitcast(FP8X4), scales, src)
+        def quantize(src, name, codes=None):
+            if codes is None:
+                codes = new([P, GROUP], U32, name + "_codes")[:]
+            scales = new([P, GROUP], U8, name + "_scales")[:]
+            nc.vector.quantize_mx(codes.bitcast(FP8X4), scales, src)
             return codes, scales
 
-        def quantize_weight(dealt, name, tag=None):
-            return quantize(dealt[:].rearrange("p t m i -> p (t m i)"), name, tag)
+        def quantize_weight(dealt, name, codes=None):
+            return quantize(dealt[:].rearrange("p t m i -> p (t m i)"), name, codes)
 
         def weave(src, dst):
             nc.scalar.copy(
                 dst.rearrange("p (c i t) -> p c t i", i=4, t=PACK),
-                src.rearrange("p (t c i) -> p c t i", i=4, t=PACK),
+                src.rearrange("p t (c i) -> p c t i", i=4),
             )
             return dst
 
@@ -105,8 +105,10 @@ def tile_list_gore_ledger_rigging_kernel(
 
         tab_s = new([P, T], U8, "tab_s")
         nc.vector.memset(tab_s[:].bitcast(I32), 0)
-        w2_s_raw = new([P, 2, H], U8, "w2_s_raw")
-        nc.vector.memset(w2_s_raw[:].rearrange("p a c -> p (a c)").bitcast(I32), 0)
+        w2_s_raw = new([P, H], U8, "w2_s_raw")
+        nc.vector.memset(w2_s_raw[:].bitcast(I32), 0)
+        w2_s1 = new([P, H], U8, "w2_s1")
+        nc.vector.memset(w2_s1[:].bitcast(I32), 0)
 
         tab_w = [new([P, T], U32, "tab_w%d" % a) for a in range(2)]
 
@@ -141,33 +143,39 @@ def tile_list_gore_ledger_rigging_kernel(
         gt_t = load_gain(gt, "gt_t")
         gz_t = load_gain(gz, "gz_t")
         pages[2] = load_page(2)
+        wg2 = load_wgs(2, 3)
         pages[3] = load_page(3)
-        wg2 = load_wgs(2, 4)
-        wg = [wg0[:, 0, :], wg1[:, 0, :], wg2[:, 0, :], wg2[:, 1, :]]
-        w2_w_raw = new([P, 2, 2 * H], U8, "w2_w_raw")
-        nc.sync.dma_start(w2_w_raw[:].bitcast(I32), w2_words.rearrange("a p c -> p a c").bitcast(I32))
-        for k in range(PACK, SLOTS):
-            pages[k] = load_page(k)
+        wg3 = load_wgs(3, 4)
+        wg = [wg0[:, 0, :], wg1[:, 0, :], wg2[:, 0, :], wg3[:, 0, :]]
 
         q1 = {}
         q3 = {}
         for a in range(2):
             q1[0, a] = quantize_weight(round_weight(raw1[0, a], "w1d_0%d" % a, "dealt%d" % a), "w1_0%d" % a)
         raw3[0, 0] = load_weight(w3, 0, 0, "stage0")
+        pages[4] = load_page(4)
+        pages[5] = load_page(5)
+        w2_w_raw = new([P, 2, 2 * H], U8, "w2_w_raw")
+        nc.sync.dma_start(w2_w_raw[:].bitcast(I32), w2_words.rearrange("a p c -> p a c").bitcast(I32))
         raw3[0, 1] = load_weight(w3, 0, 1, "stage1")
+        pages[6] = load_page(6)
+        pages[7] = load_page(7)
         idx4 = load_list(offs4, "idx4")
-        go_t = load_gain(go, "go_t")
+        second = new([P, PACK * S], F32, "opposite1")
+        go_rows = go.rearrange("(b p t) -> p b t", p=P, t=PACK)
+        go_t = new([P, PACK], F32, "go_t")
+        nc.sync.dma_start(go_t[:], go_rows[:, 1, :])
+        go_col = {PACK + t: go_t[:, t:t + 1] for t in range(PACK)}
+        for u in range(2):
+            at = (2 + u) * S
+            nc.sync.dma_start(second[:, at:at + 2], go_rows[:, 0, 2 * u:2 * u + 2])
+            for e in range(2):
+                go_col[2 * u + e] = second[:, at + e:at + e + 1]
         for q in range(4):
             nc.sync.dma_start(
-                w2_s_raw[32 * q:32 * q + 4, :, :].bitcast(I32),
-                w2_scales[:, 4 * q:4 * q + 4, :].rearrange("a r c -> r a c").bitcast(I32),
+                w2_s_raw[32 * q:32 * q + 8, :].bitcast(I32),
+                w2_scales[:, 4 * q:4 * q + 4, :].bitcast(I32),
             )
-
-        w2_s = new([P, 2, H], U8, "w2_s")
-        nc.vector.tensor_copy(
-            w2_s[:].rearrange("p a (b t o i) -> p (a b) o t i", b=2, t=PACK, i=16),
-            w2_s_raw[:].rearrange("p a (b o i t) -> p (a b) o t i", b=2, t=PACK, i=16),
-        )
 
         v_w = []
         v_s = new([P, S], U8, "v_s")
@@ -194,7 +202,10 @@ def tile_list_gore_ledger_rigging_kernel(
             nc.scalar.copy(h[k][:, js], acc)
 
         def stage1(k):
-            h[k] = new([P, S], F32, "h%d" % k)
+            if k < PACK:
+                h[k] = new([P, S], F32, "h%d" % k)[:]
+            else:
+                h[k] = raw3[0, (k - PACK) // 2][:, k % 2, :]
             if k == 0:
                 for u in range(2):
                     acc = bank(u * (SLOTS - 1), "h_acc0_%d" % u)
@@ -203,26 +214,27 @@ def tile_list_gore_ledger_rigging_kernel(
                 stage1_part(k, bank(k, "h_acc%d" % k)[:], slice(0, S), (1, 0))
 
         picked = {}
-        opposite = [new([P, PACK * S], F32, "opposite%d" % b) for b in range(2)]
+        wide = new([P, 2 * PACK * S], F32, "opposite0")
+        opposite = [wide[:].rearrange("p (t u j) -> p t u j", t=PACK, u=2)[:, :, 0, :],
+                    second[:].rearrange("p (t j) -> p t j", t=PACK)]
 
-        def lodge(half):
-            b, u = divmod(half, 2)
-            return opposite[b][:, 2 * u * S:2 * (u + 1) * S].bitcast(BF16)
+        def lodge(t):
+            return wide[:, 2 * t * S:2 * (t + 1) * S].bitcast(BF16)
 
-        t_rows = [lodge(0), new([P, PACK * S], BF16, "t_rows1", "rows1")[:]]
+        t_rows = [lodge(0).rearrange("p (t j) -> p t j", t=PACK), new([P, PACK, S], BF16, "t_rows1", "rows1")[:]]
 
         def put(k):
-            nc.vector.tensor_tensor(pages[k][:].indirect(idx2[:]), h[k][:], wg[k % PACK], ALU.mult)
+            nc.vector.tensor_tensor(pages[k][:].indirect(idx2[:]), h[k], wg[k % PACK], ALU.mult)
 
         def pick(k):
-            picked[k] = new([P, S], F32, "picked%d" % k)
+            picked[k] = new([P, S], F32, "picked%d" % k, "h%d" % k)
             nc.vector.tensor_copy(picked[k][:], pages[k][:].indirect(idx3[:]))
 
         def gate(k, tag):
             b, t = divmod(k, PACK)
-            th = new([P, S], F32, "th%d" % k, tag)
+            th = new([P, S], F32, "th%d" % k, tag) if tag else raw3[0, k // PACK][:, 2, :]
             nc.scalar.activation(th[:], picked[k][:], ACT.Tanh, scale=col(gx_t, k))
-            nc.scalar.activation(t_rows[b][:, t * S:(t + 1) * S], th[:], ACT.Copy, scale=col(gt_t, k))
+            nc.scalar.activation(t_rows[b][:, t, :], th[:], ACT.Copy, scale=col(gt_t, k))
 
         def skip(k):
             nc.scalar.activation(picked[k][:], picked[k][:], ACT.Copy, scale=col(gxz_t, k))
@@ -248,50 +260,67 @@ def tile_list_gore_ledger_rigging_kernel(
         gate(1, "stage3")
         skip(1)
         raw3[1, 1] = load_weight(w3, 1, 1, "stage3")
+        put(2)
+        pick(2)
+        put(3)
+        pick(3)
+        d3a = round_weight(raw3[0, 0], "w3d_00", "dealt0")
+        stage1(4)
+        stage1(5)
+        gate(2, None)
+        skip(2)
         w2_w = new([P, 2, 2 * H], U8, "w2_w")
         nc.scalar.copy(
             w2_w[:].bitcast(U16).rearrange("p a (b t o i) -> p (a b) o t i", b=2, t=PACK, i=8),
             w2_w_raw[:].bitcast(U16).rearrange("p a (b o i t) -> p (a b) o t i", b=2, t=PACK, i=8),
         )
-        for k in range(PACK, SLOTS):
-            stage1(k)
-        put(2)
-        put(3)
-        pick(2)
-        pick(3)
-        d3a = round_weight(raw3[0, 0], "w3d_00", "dealt0")
-        gate(2, "stage0")
-        skip(2)
-        gate(3, "stage0")
-        t_woven0 = weave(t_rows[0], new([P, PACK * S], BF16, "t_woven0", "woven0")[:])
+        d3b = round_weight(raw3[0, 1], "w3d_01", "dealt1")
+        stage1(6)
+        stage1(7)
+        gate(3, "w2_w_raw")
         skip(3)
-        d3b = round_weight(raw3[0, 1], "w3d_01", "stage0")
+        t_woven0 = weave(t_rows[0], new([P, PACK * S], BF16, "t_woven0", "woven0")[:])
         put(4)
         put(5)
         pick(4)
-        gate(4, "stage1")
-        skip(4)
-        put(6)
         pick(5)
-        gate(5, "stage1")
-        skip(5)
-        d3c = round_weight(raw3[1, 0], "w3d_10", "stage1")
+        gate(4, None)
+        gate(5, None)
+        d3c = round_weight(raw3[1, 0], "w3d_10", "w2_w_raw")
+        put(6)
         put(7)
         pick(6)
         pick(7)
         gate(6, "stage2")
-        skip(6)
         gate(7, "stage2")
         t_woven1 = weave(t_rows[1], lodge(1))
-        skip(7)
-        d3d = round_weight(raw3[1, 1], "w3d_11", "rows1")
+        late = new([P, 6, S], F32, "late", "rows1")
+        for k in range(PACK, SLOTS):
+            nc.scalar.activation(late[:, k - PACK, :], picked[k][:], ACT.Copy, scale=col(gxz_t, k))
+            picked[k] = late[:, k - PACK, :]
+        d3d = late[:, 4:6, :].rearrange("p u j -> p (u j)").bitcast(BF16)
+        nc.scalar.copy(
+            d3d.rearrange("p (t m i) -> p m i t", t=PACK, i=PACK),
+            raw3[1, 1][:].rearrange("p i (m t) -> p m i t", t=PACK),
+        )
+        w2_s0 = new([P, H], U8, "w2_s0", "wgs3")
+        nc.vector.tensor_copy(
+            w2_s0[:].rearrange("p (b t o i) -> p b o t i", b=2, t=PACK, i=16),
+            w2_s_raw[:].rearrange("p (b o i t) -> p b o t i", b=2, t=PACK, i=16),
+        )
+        for q in range(4):
+            nc.sync.dma_start(
+                w2_s1[32 * q:32 * q + 4, :].bitcast(I32), w2_s0[32 * q + 4:32 * q + 8, :].bitcast(I32))
+        w2_s = [w2_s0, w2_s1]
         qt = [quantize(t_woven0, "t0")]
-        q3[0, 0] = quantize_weight(d3a, "w3_00")
-        q3[0, 1] = quantize_weight(d3b, "w3_01")
+        w3_codes = new([P, 2, GROUP], U32, "w3_0_codes", "stage1")
+        q3[0, 0] = quantize_weight(d3a, "w3_00", w3_codes[:, 0, :])
+        q3[0, 1] = quantize_weight(d3b, "w3_01", w3_codes[:, 1, :])
+        q3[1, 0] = quantize_weight(d3c, "w3_10")
 
         def pick_opposite(k):
             b, t = divmod(k, PACK)
-            nc.vector.tensor_copy(opposite[b][:, t * S:(t + 1) * S], pages[k][:].indirect(idx4[:]))
+            nc.vector.tensor_copy(opposite[b][:, t, :], pages[k][:].indirect(idx4[:]))
 
         s_acc = [bank(k, "s_acc%d" % k) for k in range(SLOTS)]
 
@@ -299,7 +328,7 @@ def tile_list_gore_ledger_rigging_kernel(
             codes, scales = qt[a]
             nc.tensor.matmul_mx(
                 s_acc[k][:], lhsT=w2_w[:, a, 2 * k * P:2 * (k + 1) * P].bitcast(FP4X4),
-                lhsT_scale=w2_s[:, a, k * P:(k + 1) * P],
+                lhsT_scale=w2_s[a][:, k * P:(k + 1) * P],
                 rhs=codes[:].bitcast(FP8X4), rhs_scale=scales,
                 start=(a == 0), stop=(a == 1),
             )
@@ -307,25 +336,25 @@ def tile_list_gore_ledger_rigging_kernel(
         for k in range(SLOTS):
             stage2(k, 0)
         pick_opposite(0)
-        pick_opposite(1)
-        q3[1, 0] = quantize_weight(d3c, "w3_10")
         qt.append(quantize(t_woven1, "t1"))
-        pick_opposite(2)
-        pick_opposite(3)
+        pick_opposite(1)
         for k in range(SLOTS):
             stage2(k, 1)
 
-        z_rows = [lodge(2), lodge(3)]
+        z_rows = [
+            wide[:, PACK * S:].bitcast(BF16).rearrange("p (t u j) -> p t u j", t=PACK, u=2)[:, :, 0, :],
+            second[:, 0:2 * S].bitcast(BF16).rearrange("p (t j) -> p t j", t=PACK),
+        ]
         z_woven = []
         for b in range(2):
             for t in range(PACK):
                 k = b * PACK + t
                 nc.vector.scalar_tensor_tensor(
-                    z_rows[b][:, t * S:(t + 1) * S], s_acc[k][:], col(gz_t, k), picked[k][:], ALU.mult, ALU.add,
+                    z_rows[b][:, t, :], s_acc[k][:], col(gz_t, k), picked[k][:], ALU.mult, ALU.add,
                 )
             z_woven.append(weave(z_rows[b], new([P, PACK * S], BF16, "z_woven%d" % b, "woven%d" % b)[:]))
 
-        q3[1, 1] = quantize_weight(d3d, "w3_11")
+        q3[1, 1] = quantize(d3d, "w3_11")
 
         y_acc = [bank(k, "y_acc%d" % k) for k in range(SLOTS)]
         qz = []
@@ -342,21 +371,21 @@ def tile_list_gore_ledger_rigging_kernel(
 
         for a in range(2):
             qz.append(quantize(z_woven[a], "z%d" % a))
+            pick_opposite(2 + 2 * a)
+            pick_opposite(3 + 2 * a)
             for k in range(SLOTS):
                 stage3(k, a)
-        for k in range(PACK, SLOTS):
-            pick_opposite(k)
 
         y_scales = new([P, 2, S], U8, "y_scales")
         y_codes = [new([P, S], U32, "y_codes%d" % b) for b in range(2)]
 
         def finish(b, j0, j1, engine_copy, tag):
             rows = out_0[b * GROUP:(b + 1) * GROUP, :].rearrange("(p t) j -> p t j", t=PACK)
-            y = opposite[b][:].rearrange("p (t j) -> p t j", t=PACK)[:, :, j0:j1]
+            y = opposite[b][:, :, j0:j1]
             for t in range(PACK):
                 k = b * PACK + t
                 nc.vector.scalar_tensor_tensor(
-                    y[:, t, :], y[:, t, :], col(go_t, k), y_acc[k][:, j0:j1], ALU.mult, ALU.max)
+                    y[:, t, :], y[:, t, :], go_col[k], y_acc[k][:, j0:j1], ALU.mult, ALU.max)
                 if j1 - j0 == S:
                     nc.sync.dma_start(rows[:, t, :], y[:, t, :])
             if j1 - j0 < S:
@@ -372,7 +401,9 @@ def tile_list_gore_ledger_rigging_kernel(
             nc.sync.dma_start(
                 out_1[b].rearrange("p m t -> p (m t)").bitcast(I32)[:, j0:j1], y_codes[b][:, j0:j1].bitcast(I32))
 
-        finish(0, 0, S, nc.scalar.copy, "woven0")
+        finish(0, 0, S, nc.scalar.copy, "dealt0")
+        pick_opposite(6)
+        pick_opposite(7)
         finish(1, 0, S // 2, nc.scalar.copy, "woven1")
         finish(1, S // 2, S, nc.vector.tensor_copy, "woven2")
         for q in range(4):

from contextlib import ExitStack

import concourse.mybir as mybir

K, T, S, H, T2 = 1024, 2048, 512, 1024, 1024
FLOPS = 3 * 2 * H * H * S

F32 = mybir.dt.float32
BF16 = mybir.dt.bfloat16
I32 = mybir.dt.int32
U32 = mybir.dt.uint32
U16 = mybir.dt.uint16
U8 = mybir.dt.uint8
FP8X4 = mybir.dt.float8_e4m3fn_x4
FP4X4 = mybir.dt.float4_e2m1fn_x4
ALU = mybir.AluOpType
ACT = mybir.ActivationFunctionType

P = 128
PACK = 4
GROUP = P * PACK
SLOTS = H // P


def tile_list_gore_ledger_rigging_kernel(
    tc, tab_words, tab_scales, offs, w1, wgs, page0, offs2, offs3, offs4,
    gx, gt, w2_words, w2_scales, gz, w3, go, out_0, out_1, out_2,
):
    nc = tc.nc
    with ExitStack() as ctx:
        lists = ctx.enter_context(tc.tile_pool(name="lists", bufs=1))
        sb = ctx.enter_context(tc.tile_pool(name="sb", bufs=1))
        psum = ctx.enter_context(tc.psum_pool(name="psum", bufs=1))

        def new(shape, dtype, name, tag=None):
            return sb.tile(shape, dtype, name=name, tag=tag or name, align_bytes=64)

        def bank(k, name):
            return psum.tile([P, S], F32, name=name, tag="bank%d" % k)

        def load_list(src, name):
            dst = lists.tile([P, S // 16], U16, name=name)
            nc.sync.dma_start(dst[:], src)
            return dst

        def load_weight(w, b, a, tag):
            raw = new([P, PACK, GROUP], F32, "raw_%s_%d%d" % (tag, b, a), tag)
            src = w[a * GROUP:(a + 1) * GROUP, b * GROUP:(b + 1) * GROUP].rearrange("(p i) c -> p i c", i=PACK)
            nc.sync.dma_start(raw[:], src)
            return raw

        def round_weight(raw, name, tag):
            dealt = new([P, PACK, P, PACK], BF16, name, tag)
            nc.scalar.copy(
                dealt[:].rearrange("p t m i -> p m i t"),
                raw[:].rearrange("p i (m t) -> p m i t", t=PACK),
            )
            return dealt

        def quantize(src, name, codes=None):
            if codes is None:
                codes = new([P, GROUP], U32, name + "_codes")[:]
            scales = new([P, GROUP], U8, name + "_scales")[:]
            nc.vector.quantize_mx(codes.bitcast(FP8X4), scales, src)
            return codes, scales

        def quantize_weight(dealt, name, codes=None):
            return quantize(dealt[:].rearrange("p t m i -> p (t m i)"), name, codes)

        def weave(src, dst):
            nc.scalar.copy(
                dst.rearrange("p (c i t) -> p c t i", i=4, t=PACK),
                src.rearrange("p t (c i) -> p c t i", i=4),
            )
            return dst

        def load_page(k):
            b, t = divmod(k, PACK)
            page = new([P, T2], F32, "page%d" % k)
            rows = page0[b * GROUP:(b + 1) * GROUP, :].rearrange("(p t) c -> p t c", t=PACK)
            nc.sync.dma_start(page[:], rows[:, t, :])
            return page

        def load_wgs(t0, t1):
            dst = new([P, t1 - t0, S], F32, "wgs%d" % t0)
            rows = wgs.rearrange("(p t) j -> p t j", t=PACK)
            for q in (0, 2, 1, 3):
                nc.sync.dma_start(dst[32 * q:32 * (q + 1), :, :], rows[:, t0:t1, :])
            return dst

        def load_gain(vec, name):
            dst = new([P, 2, PACK], F32, name)
            nc.sync.dma_start(dst[:], vec.rearrange("(b p t) -> p b t", p=P, t=PACK))
            return dst

        def col(gain, k):
            b, t = divmod(k, PACK)
            return gain[:, b, t:t + 1]

        def entries(u):
            return slice(u * S // 2, (u + 1) * S // 2)

        def columns(u):
            return slice(u * S // 32, (u + 1) * S // 32)

        tab_s = new([P, T], U8, "tab_s")
        nc.vector.memset(tab_s[:].bitcast(I32), 0)
        w2_s_raw = new([P, H], U8, "w2_s_raw")
        nc.vector.memset(w2_s_raw[:].bitcast(I32), 0)
        w2_s1 = new([P, H], U8, "w2_s1")
        nc.vector.memset(w2_s1[:].bitcast(I32), 0)

        tab_w = [new([P, T], U32, "tab_w%d" % a) for a in range(2)]

        def load_tab(a):
            nc.sync.dma_start(
                tab_w[a][:].bitcast(I32),
                tab_words[a].rearrange("p n t -> p (n t)").bitcast(I32),
            )

        raw1 = {}
        raw3 = {}
        pages = {}
        raw1[0, 0] = load_weight(w1, 0, 0, "stage0")
        tab_s_rows = new([P, T // 4], I32, "tab_s_rows")
        for q in range(4):
            live = slice(32 * q, 32 * q + 8)
            nc.sync.dma_start(tab_s_rows[live, :], tab_scales[:, 4 * q:4 * q + 4, :].bitcast(I32))
            nc.vector.tensor_copy(tab_s[live, :].bitcast(I32), tab_s_rows[live, :])
        idx = load_list(offs, "idx")
        raw1[0, 1] = load_weight(w1, 0, 1, "stage1")
        load_tab(0)
        load_tab(1)
        idx2 = load_list(offs2, "idx2")
        wg0 = load_wgs(0, 1)
        pages[0] = load_page(0)
        pages[1] = load_page(1)
        wg1 = load_wgs(1, 2)
        idx3 = load_list(offs3, "idx3")
        raw1[1, 0] = load_weight(w1, 1, 0, "stage2")
        gx_t = load_gain(gx, "gx_t")
        raw1[1, 1] = load_weight(w1, 1, 1, "stage3")
        gt_t = load_gain(gt, "gt_t")
        gz_t = load_gain(gz, "gz_t")
        pages[2] = load_page(2)
        wg2 = load_wgs(2, 3)
        pages[3] = load_page(3)
        wg3 = load_wgs(3, 4)
        wg = [wg0[:, 0, :], wg1[:, 0, :], wg2[:, 0, :], wg3[:, 0, :]]

        q1 = {}
        q3 = {}
        for a in range(2):
            q1[0, a] = quantize_weight(round_weight(raw1[0, a], "w1d_0%d" % a, "dealt%d" % a), "w1_0%d" % a)
        raw3[0, 0] = load_weight(w3, 0, 0, "stage0")
        pages[4] = load_page(4)
        pages[5] = load_page(5)
        w2_w_raw = new([P, 2, 2 * H], U8, "w2_w_raw")
        nc.sync.dma_start(w2_w_raw[:].bitcast(I32), w2_words.rearrange("a p c -> p a c").bitcast(I32))
        raw3[0, 1] = load_weight(w3, 0, 1, "stage1")
        pages[6] = load_page(6)
        pages[7] = load_page(7)
        idx4 = load_list(offs4, "idx4")
        second = new([P, PACK * S], F32, "opposite1")
        go_rows = go.rearrange("(b p t) -> p b t", p=P, t=PACK)
        go_t = new([P, PACK], F32, "go_t")
        nc.sync.dma_start(go_t[:], go_rows[:, 1, :])
        go_col = {PACK + t: go_t[:, t:t + 1] for t in range(PACK)}
        for u in range(2):
            at = (2 + u) * S
            nc.sync.dma_start(second[:, at:at + 2], go_rows[:, 0, 2 * u:2 * u + 2])
            for e in range(2):
                go_col[2 * u + e] = second[:, at + e:at + e + 1]
        for q in range(4):
            nc.sync.dma_start(
                w2_s_raw[32 * q:32 * q + 8, :].bitcast(I32),
                w2_scales[:, 4 * q:4 * q + 4, :].bitcast(I32),
            )

        v_w = []
        v_s = new([P, S], U8, "v_s")
        for a in range(2):
            words = new([P, S], U32, "v_w%d" % a)
            v_w.append(words)
        nc.vector.tensor_copy(v_s[:], tab_s[:].indirect(idx[:]))
        nc.vector.tensor_copy(v_w[0][:], tab_w[0][:].indirect(idx[:]))
        for u in range(2):
            nc.vector.tensor_copy(v_w[1][:, entries(u)], tab_w[1][:].indirect(idx[:, columns(u)]))

        h = {}

        def stage1_part(k, acc, js, order):
            b, t = divmod(k, PACK)
            cols = slice(t * P, (t + 1) * P)
            for a in order:
                codes, scales = q1[b, a]
                nc.tensor.matmul_mx(
                    acc, lhsT=codes[:, cols].bitcast(FP8X4), lhsT_scale=scales[:, cols],
                    rhs=v_w[a][:, js].bitcast(FP8X4), rhs_scale=v_s[4 * a:P, js],
                    start=(a == order[0]), stop=(a == order[1]),
                )
            nc.scalar.copy(h[k][:, js], acc)

        def stage1(k):
            if k < PACK:
                h[k] = new([P, S], F32, "h%d" % k)[:]
            else:
                h[k] = raw3[0, (k - PACK) // 2][:, k % 2, :]
            if k == 0:
                for u in range(2):
                    acc = bank(u * (SLOTS - 1), "h_acc0_%d" % u)
                    stage1_part(0, acc[:, 0:S // 2], entries(u), (0, 1))
            else:
                stage1_part(k, bank(k, "h_acc%d" % k)[:], slice(0, S), (1, 0))

        picked = {}
        wide = new([P, 2 * PACK * S], F32, "opposite0")
        opposite = [wide[:].rearrange("p (t u j) -> p t u j", t=PACK, u=2)[:, :, 0, :],
                    second[:].rearrange("p (t j) -> p t j", t=PACK)]

        def lodge(t):
            return wide[:, 2 * t * S:2 * (t + 1) * S].bitcast(BF16)

        t_rows = [lodge(0).rearrange("p (t j) -> p t j", t=PACK), new([P, PACK, S], BF16, "t_rows1", "rows1")[:]]

        def put(k):
            nc.vector.tensor_tensor(pages[k][:].indirect(idx2[:]), h[k], wg[k % PACK], ALU.mult)

        def pick(k):
            picked[k] = new([P, S], F32, "picked%d" % k, "h%d" % k)
            nc.vector.tensor_copy(picked[k][:], pages[k][:].indirect(idx3[:]))

        def gate(k, tag):
            b, t = divmod(k, PACK)
            th = new([P, S], F32, "th%d" % k, tag) if tag else raw3[0, k // PACK][:, 2, :]
            nc.scalar.activation(th[:], picked[k][:], ACT.Tanh, scale=col(gx_t, k))
            nc.scalar.activation(t_rows[b][:, t, :], th[:], ACT.Copy, scale=col(gt_t, k))

        def skip(k):
            nc.scalar.activation(picked[k][:], picked[k][:], ACT.Copy, scale=col(gxz_t, k))

        for k in range(PACK):
            stage1(k)

        d10 = round_weight(raw1[1, 0], "w1d_10", "dealt0")
        d11 = round_weight(raw1[1, 1], "w1d_11", "dealt1")
        for u in range(2):
            nc.vector.tensor_tensor(
                pages[0][:].indirect(idx2[:, columns(u)]), h[0][:, entries(u)], wg[0][:, entries(u)], ALU.mult)
        put(1)
        pick(0)
        pick(1)
        gxz_t = new([P, 2, PACK], F32, "gxz_t")
        nc.vector.tensor_tensor(gxz_t[:], gx_t[:], gz_t[:], ALU.mult)
        q1[1, 0] = quantize_weight(d10, "w1_10")
        q1[1, 1] = quantize_weight(d11, "w1_11")
        gate(0, "stage2")
        skip(0)
        raw3[1, 0] = load_weight(w3, 1, 0, "stage2")
        gate(1, "stage3")
        skip(1)
        raw3[1, 1] = load_weight(w3, 1, 1, "stage3")
        put(2)
        pick(2)
        put(3)
        pick(3)
        d3a = round_weight(raw3[0, 0], "w3d_00", "dealt0")
        stage1(4)
        stage1(5)
        gate(2, None)
        skip(2)
        w2_w = new([P, 2, 2 * H], U8, "w2_w")
        nc.scalar.copy(
            w2_w[:].bitcast(U16).rearrange("p a (b t o i) -> p (a b) o t i", b=2, t=PACK, i=8),
            w2_w_raw[:].bitcast(U16).rearrange("p a (b o i t) -> p (a b) o t i", b=2, t=PACK, i=8),
        )
        d3b = round_weight(raw3[0, 1], "w3d_01", "dealt1")
        stage1(6)
        stage1(7)
        gate(3, "w2_w_raw")
        skip(3)
        t_woven0 = weave(t_rows[0], new([P, PACK * S], BF16, "t_woven0", "woven0")[:])
        put(4)
        put(5)
        pick(4)
        pick(5)
        gate(4, None)
        gate(5, None)
        d3c = round_weight(raw3[1, 0], "w3d_10", "w2_w_raw")
        put(6)
        put(7)
        pick(6)
        pick(7)
        gate(6, "stage2")
        gate(7, "stage2")
        t_woven1 = weave(t_rows[1], lodge(1))
        late = new([P, 6, S], F32, "late", "rows1")
        for k in range(PACK, SLOTS):
            nc.scalar.activation(late[:, k - PACK, :], picked[k][:], ACT.Copy, scale=col(gxz_t, k))
            picked[k] = late[:, k - PACK, :]
        d3d = late[:, 4:6, :].rearrange("p u j -> p (u j)").bitcast(BF16)
        nc.scalar.copy(
            d3d.rearrange("p (t m i) -> p m i t", t=PACK, i=PACK),
            raw3[1, 1][:].rearrange("p i (m t) -> p m i t", t=PACK),
        )
        w2_s0 = new([P, H], U8, "w2_s0", "wgs3")
        nc.vector.tensor_copy(
            w2_s0[:].rearrange("p (b t o i) -> p b o t i", b=2, t=PACK, i=16),
            w2_s_raw[:].rearrange("p (b o i t) -> p b o t i", b=2, t=PACK, i=16),
        )
        for q in range(4):
            nc.sync.dma_start(
                w2_s1[32 * q:32 * q + 4, :].bitcast(I32), w2_s0[32 * q + 4:32 * q + 8, :].bitcast(I32))
        w2_s = [w2_s0, w2_s1]
        qt = [quantize(t_woven0, "t0")]
        w3_codes = new([P, 2, GROUP], U32, "w3_0_codes", "stage1")
        q3[0, 0] = quantize_weight(d3a, "w3_00", w3_codes[:, 0, :])
        q3[0, 1] = quantize_weight(d3b, "w3_01", w3_codes[:, 1, :])
        q3[1, 0] = quantize_weight(d3c, "w3_10")

        def pick_opposite(k):
            b, t = divmod(k, PACK)
            nc.vector.tensor_copy(opposite[b][:, t, :], pages[k][:].indirect(idx4[:]))

        s_acc = [bank(k, "s_acc%d" % k) for k in range(SLOTS)]

        def stage2(k, a):
            codes, scales = qt[a]
            nc.tensor.matmul_mx(
                s_acc[k][:], lhsT=w2_w[:, a, 2 * k * P:2 * (k + 1) * P].bitcast(FP4X4),
                lhsT_scale=w2_s[a][:, k * P:(k + 1) * P],
                rhs=codes[:].bitcast(FP8X4), rhs_scale=scales,
                start=(a == 0), stop=(a == 1),
            )

        for k in range(SLOTS):
            stage2(k, 0)
        pick_opposite(0)
        qt.append(quantize(t_woven1, "t1"))
        pick_opposite(1)
        for k in range(SLOTS):
            stage2(k, 1)

        z_rows = [
            wide[:, PACK * S:].bitcast(BF16).rearrange("p (t u j) -> p t u j", t=PACK, u=2)[:, :, 0, :],
            second[:, 0:2 * S].bitcast(BF16).rearrange("p (t j) -> p t j", t=PACK),
        ]
        z_woven = []
        for b in range(2):
            for t in range(PACK):
                k = b * PACK + t
                nc.vector.scalar_tensor_tensor(
                    z_rows[b][:, t, :], s_acc[k][:], col(gz_t, k), picked[k][:], ALU.mult, ALU.add,
                )
            z_woven.append(weave(z_rows[b], new([P, PACK * S], BF16, "z_woven%d" % b, "woven%d" % b)[:]))

        q3[1, 1] = quantize(d3d, "w3_11")

        y_acc = [bank(k, "y_acc%d" % k) for k in range(SLOTS)]
        qz = []

        def stage3(k, a):
            b, t = divmod(k, PACK)
            cols = slice(t * P, (t + 1) * P)
            codes, scales = q3[b, a]
            nc.tensor.matmul_mx(
                y_acc[k][:], lhsT=codes[:, cols].bitcast(FP8X4), lhsT_scale=scales[:, cols],
                rhs=qz[a][0][:].bitcast(FP8X4), rhs_scale=qz[a][1],
                start=(a == 0), stop=(a == 1),
            )

        for a in range(2):
            qz.append(quantize(z_woven[a], "z%d" % a))
            pick_opposite(2 + 2 * a)
            pick_opposite(3 + 2 * a)
            for k in range(SLOTS):
                stage3(k, a)

        y_scales = new([P, 2, S], U8, "y_scales")
        y_codes = [new([P, S], U32, "y_codes%d" % b) for b in range(2)]

        def finish(b, j0, j1, engine_copy, tag):
            rows = out_0[b * GROUP:(b + 1) * GROUP, :].rearrange("(p t) j -> p t j", t=PACK)
            y = opposite[b][:, :, j0:j1]
            for t in range(PACK):
                k = b * PACK + t
                nc.vector.scalar_tensor_tensor(
                    y[:, t, :], y[:, t, :], go_col[k], y_acc[k][:, j0:j1], ALU.mult, ALU.max)
                if j1 - j0 == S:
                    nc.sync.dma_start(rows[:, t, :], y[:, t, :])
            if j1 - j0 < S:
                nc.sync.dma_start(rows[:, :, j0:j1], y)
            woven = new([P, j1 - j0, PACK], BF16, "y_woven%d_%d" % (b, j0), tag)
            engine_copy(
                woven[:].rearrange("p (c i) t -> p c t i", i=4),
                y.rearrange("p t (c i) -> p c t i", i=4),
            )
            nc.vector.quantize_mx(
                y_codes[b][:, j0:j1].bitcast(FP8X4), y_scales[:, b, j0:j1],
                woven[:].rearrange("p j t -> p (j t)"))
            nc.sync.dma_start(
                out_1[b].rearrange("p m t -> p (m t)").bitcast(I32)[:, j0:j1], y_codes[b][:, j0:j1].bitcast(I32))

        finish(0, 0, S, nc.scalar.copy, "dealt0")
        pick_opposite(6)
        pick_opposite(7)
        finish(1, 0, S // 2, nc.scalar.copy, "woven1")
        finish(1, S // 2, S, nc.vector.tensor_copy, "woven2")
        for q in range(4):
            nc.sync.dma_start(
                out_2[:, 4 * q:4 * q + 4, :].rearrange("g r m -> r g m").bitcast(I32),
                y_scales[32 * q:32 * q + 4, :, :].bitcast(I32),
            )
